import numpy as np
import ml_dtypes


def mxq(x, axis, fmt="e4m3"):
    dtype, down = {"e4m3": (ml_dtypes.float8_e4m3fn, 7), "e5m2": (ml_dtypes.float8_e5m2, 14)}[fmt]
    v = np.moveaxis(np.asarray(x, np.float32).astype(ml_dtypes.bfloat16).astype(np.float64), axis, -1)
    blocks = v.reshape(v.shape[:-1] + (-1, 32))
    amax = np.abs(blocks).max(-1, keepdims=True)
    byte = np.maximum(np.where(amax > 0, np.frexp(amax)[1] - 1 + 127, 0) - down, 1)
    scale = np.exp2(byte - 127.0)
    codes = (blocks / scale).astype(np.float32).astype(dtype).astype(np.float64)
    return np.moveaxis((codes * scale).reshape(v.shape), -1, axis)


WIDE = False


def mx_kscale(k):
    if not WIDE:
        return np.ones(k)
    levels = np.array([10, -10, 5, -5, 0])
    if k % 512:
        return np.exp2(np.random.permutation(np.resize(levels, k // 32))).repeat(32)
    a = np.empty((k // 512, 16))
    for p in range(k // 512):
        a[p, :8] = np.random.permutation(np.resize(levels, 8))
        for g in range(8):
            far = levels[np.abs(levels - a[p, g]) >= 10]
            a[p, g + 8] = far[np.random.randint(len(far))]
    return np.exp2(a.ravel()).repeat(32)


def f64(x):
    return np.asarray(x).astype(np.float64)


def striped(idx):
    return np.tile(np.asarray(idx).reshape(-1, 16).T, (8, 1)).astype(np.uint16)


def unstriped(offs):
    return offs[:16].T.reshape(-1).astype(np.int64)


E2M1 = np.array([0.0, 0.5, 1.0, 1.5, 2.0, 3.0, 4.0, 6.0, -0.0, -0.5, -1.0, -1.5, -2.0, -3.0, -4.0, -6.0])


def pack_weight(w, fmt):
    k, n = w.shape
    w = f64(np.asarray(w, np.float32).astype(ml_dtypes.bfloat16)).reshape(k // 32, 32, n)
    amax = np.abs(w).max(1)
    if fmt == "e4m3":
        byte = np.frexp(amax)[1] - 1 + 127 - 7
    else:
        mant, ex = np.frexp(amax / 6.0)
        byte = np.where(mant > 0.5, ex, ex - 1) + 127
    byte = np.clip(np.where(amax > 0, byte, 1), 1, 254)
    scaled = (w * np.exp2(127.0 - byte)[:, None, :]).reshape(k, n).astype(np.float32)
    by_word = np.ascontiguousarray(scaled.reshape(k // 512, 128, 4, n).transpose(0, 1, 3, 2))
    if fmt == "e4m3":
        words = by_word.astype(ml_dtypes.float8_e4m3fn).view(np.uint8)
    else:
        c = by_word.astype(ml_dtypes.float4_e2m1fn).view(np.uint8) & 0xF
        words = (c[..., 0::2] | (c[..., 1::2] << 4)).reshape(k // 512, 128, 2 * n)
    return np.ascontiguousarray(words), np.ascontiguousarray(byte.astype(np.uint8).reshape(k // 512, 16, n))


def unpack_weight(words, scales, fmt):
    g, _, n = scales.shape
    words = np.ascontiguousarray(words).reshape(g, 128, n, -1)
    if fmt == "e4m3":
        vals = words.view(ml_dtypes.float8_e4m3fn).astype(np.float64)
    else:
        nib = np.empty((g, 128, n, 4), np.uint8)
        nib[..., 0::2] = words & 0xF
        nib[..., 1::2] = words >> 4
        vals = E2M1[nib]
    vals = vals * np.repeat(np.exp2(scales.astype(np.float64) - 127.0), 8, axis=1)[..., None]
    return vals.transpose(0, 1, 3, 2).reshape(g * 512, n)


def sigmoid(v):
    return 1.0 / (1.0 + np.exp(-v))


D, T, I, Q, E = 512, 2048, 512, 128, 512


def setup_inputs():
    n = np.random.standard_normal
    idx = np.random.permutation(T)[:I]
    fd = mx_kscale(D)
    fi = mx_kscale(I)
    ti = np.ones(T)
    ti[idx] = fi
    keysp = pack_weight(n((D, T)) / fd[:, None], "e4m3")
    return {
        "query": (n((D, Q)) * 0.4 / np.sqrt(D) * fd[:, None]).astype(np.float32),
        "keys_words": keysp[0],
        "keys_scales": keysp[1],
        "size": (np.random.uniform(8.0, 24.0, (1, I)) * fi).astype(np.float32),
        "vals": (n((E, T)) / ti).astype(np.float32),
        "gval": (n((E, T)) / ti).astype(np.float32),
        "offs": striped(idx),
    }


def reference(query, keys_words, keys_scales, size, vals, gval, offs):
    idx = unstriped(offs)
    keysu = unpack_weight(keys_words, keys_scales, "e4m3")
    queryq = mxq(f64(query), 0, "e4m3")
    keysidxg = keysu[:, idx]
    a = queryq.T @ keysidxg
    p = np.exp(a - np.max(a, axis=1, keepdims=True))
    w = p * f64(size) / np.sum(p, axis=1, keepdims=True)
    wt = w.T
    vt = f64(vals)[:, idx].T
    ut = f64(gval)[:, idx].T
    wtq = mxq(wt, 0, "e4m3")
    vtq = mxq(vt, 0, "e4m3")
    o = wtq.T @ vtq
    utq = mxq(ut, 0, "e4m3")
    u = wtq.T @ utq
    y = o * sigmoid(u)
    return y

@@ -1,0 +1,151 @@
+from contextlib import ExitStack
+
+import concourse.mybir as mybir
+from concourse.masks import make_identity
+
+D, T, I, Q, E = 512, 2048, 512, 128, 512
+FLOPS = 2 * Q * I * (D + 2 * E)
+
+F32 = mybir.dt.float32
+BF16 = mybir.dt.bfloat16
+I32 = mybir.dt.int32
+U32 = mybir.dt.uint32
+U16 = mybir.dt.uint16
+U8 = mybir.dt.uint8
+FP8X4 = mybir.dt.float8_e4m3fn_x4
+ACT = mybir.ActivationFunctionType
+ALU = mybir.AluOpType
+
+P = 128
+PACK = 4
+BLOCKS = E // P
+ALIGN = 64
+
+
+def tile_attend_gatedvalues_kernel(tc, query, keys_words, keys_scales, size, vals, gval, offs, out):
+    nc = tc.nc
+    with ExitStack() as ctx:
+        keep = ctx.enter_context(tc.tile_pool(name="keep", bufs=1))
+        pools = ctx.enter_context(tc.tile_pool(name="pools", bufs=1))
+        last = ctx.enter_context(tc.tile_pool(name="last", bufs=1))
+        ring = ctx.enter_context(tc.tile_pool(name="ring", bufs=2))
+        psum = ctx.enter_context(tc.psum_pool(name="psum", bufs=1))
+        turn = ctx.enter_context(tc.psum_pool(name="turn", bufs=2))
+
+        offsets = keep.tile([P, I // 16], U16, name="offsets")
+        nc.sync.dma_start(offsets[:], offs)
+
+        key_pool = keep.tile([P, T], U32, name="key_pool")
+        nc.sync.dma_start(key_pool[:].bitcast(I32), keys_words.rearrange("z p n t -> p (z n t)").bitcast(I32))
+        q_raw = keep.tile([P, PACK, Q], F32, name="q_raw")
+        nc.sync.dma_start(q_raw[:], query.rearrange("(p j) q -> p j q", j=PACK))
+
+        size_col = keep.tile([P, PACK], F32, name="size_col")
+        nc.scalar.dma_start(size_col[:], size.rearrange("o (p t) -> p (o t)", t=PACK))
+        scale_pool = keep.tile([P, T], U8, name="scale_pool")
+        nc.vector.memset(scale_pool[:].bitcast(I32), 0)
+        for quad in range(4):
+            nc.scalar.dma_start(
+                scale_pool[32 * quad : 32 * quad + 4, :].bitcast(I32),
+                keys_scales[0, 4 * quad : 4 * quad + 4, :].bitcast(I32),
+            )
+
+        windows = []
+        for n in range(2 * BLOCKS):
+            source = gval if n < BLOCKS else vals
+            rows = source[(n % BLOCKS) * P : (n % BLOCKS + 1) * P, :]
+            if n == 2 * BLOCKS - 1:
+                window = last.tile([P, T], F32, name="window_last", offset=0, align_bytes=ALIGN)
+            else:
+                window = pools.tile([P, T], F32, name="window%d" % n, tag="window%d" % n, align_bytes=ALIGN)
+            nc.sync.dma_start(window[:], rows)
+            windows.append(window)
+
+        ident = keep.tile([P, P], F32, name="ident")
+        make_identity(nc, ident[:])
+
+        q_grouped = keep.tile([P, Q, PACK], BF16, name="q_grouped", align_bytes=ALIGN)
+        nc.vector.tensor_copy(q_grouped[:], q_raw[:].rearrange("p j q -> p q j"))
+        q_codes = keep.tile([P, Q], U32, name="q_codes", align_bytes=ALIGN)
+        q_scales = keep.tile([P, Q], U8, name="q_scales", align_bytes=ALIGN)
+        nc.vector.quantize_mx(q_codes[:].bitcast(FP8X4), q_scales[:], q_grouped[:].rearrange("p q j -> p (q j)"))
+
+        k_codes = keep.tile([P, I], U32, name="k_codes", align_bytes=ALIGN)
+        nc.vector.tensor_copy(k_codes[:], key_pool[:].indirect(offsets[:]))
+        k_scales = keep.tile([P, I], U8, name="k_scales", align_bytes=ALIGN)
+        nc.vector.tensor_copy(k_scales[:], scale_pool[:].indirect(offsets[:]))
+
+        scores = psum.tile([P, I], F32, name="scores", tag="soft")
+        nc.tensor.matmul_mx(scores[:], q_codes[:].bitcast(FP8X4), q_scales[:], k_codes[:].bitcast(FP8X4), k_scales[:],
+                            start=True, stop=True)
+        neg_max = keep.tile([P, 1], F32, name="neg_max")
+        nc.vector.tensor_reduce(neg_max[:], scores[:], mybir.AxisListType.X, ALU.max, negate=True)
+        expo = keep.tile([P, PACK, P], F32, name="expo")
+        row_sum = keep.tile([P, 1], F32, name="row_sum")
+        nc.scalar.activation(expo[:], scores[:].rearrange("q (s t) -> q t s", t=PACK), ACT.Exp, bias=neg_max[:],
+                             accum_out=row_sum[:])
+        inv_sum = keep.tile([P, 1], F32, name="inv_sum")
+        nc.vector.reciprocal(inv_sum[:], row_sum[:])
+        prob = keep.tile([P, PACK, P], F32, name="prob")
+        nc.scalar.activation(prob[:], expo[:], ACT.Copy, scale=inv_sum[:])
+        prob_t = psum.tile([P, PACK, Q], F32, name="prob_t", tag="soft")
+        for t in range(PACK):
+            nc.tensor.transpose(prob_t[:, t, :], prob[:, t, :], ident[:])
+        w_grouped = keep.tile([P, Q, PACK], BF16, name="w_grouped", align_bytes=ALIGN)
+        nc.vector.tensor_tensor(w_grouped[:], prob_t[:].rearrange("s t q -> s q t"),
+                                size_col[:].unsqueeze(1).to_broadcast([P, Q, PACK]), ALU.mult)
+        w_codes = keep.tile([P, Q], U32, name="w_codes", align_bytes=ALIGN)
+        w_scales = keep.tile([P, Q], U8, name="w_scales", align_bytes=ALIGN)
+        nc.vector.quantize_mx(w_codes[:].bitcast(FP8X4), w_scales[:], w_grouped[:].rearrange("p q j -> p (q j)"))
+
+        def gather_and_turn(n, grouped):
+            picked = ring.tile([P, I], BF16, name="picked")
+            nc.vector.tensor_copy(picked[:], windows[n][:].indirect(offsets[:]))
+            words = picked[:].bitcast(F32)
+            turned = turn.tile([P, 2, P], F32, name="turned")
+            for u in range(2):
+                nc.tensor.transpose(turned[:, u, :], words[:, u : I // 2 : 2], ident[:])
+            nc.scalar.copy(grouped.bitcast(F32).rearrange("s (e u) -> s e u", u=2), turned[:].rearrange("s u e -> s e u"))
+
+        def multiply(sums, grouped, codes, scales):
+            nc.vector.quantize_mx(codes.bitcast(FP8X4), scales, grouped)
+            nc.tensor.matmul_mx(sums, w_codes[:].bitcast(FP8X4), w_scales[:], codes.bitcast(FP8X4), scales,
+                                start=True, stop=True)
+
+        g_grouped = keep.tile([P, E * PACK], BF16, name="g_grouped", align_bytes=ALIGN)
+        for n in range(BLOCKS):
+            gather_and_turn(n, g_grouped[:, n * P * PACK : (n + 1) * P * PACK])
+
+        v_grouped = [keep.tile([P, P * PACK], BF16, name="v_grouped%d" % b, align_bytes=ALIGN) for b in range(BLOCKS)]
+        v_scales = [keep.tile([P, P], U8, name="v_scales%d" % b, align_bytes=ALIGN) for b in range(BLOCKS)]
+        early = psum.tile([P, 2 * P], F32, name="early")
+        third = psum.tile([P, P], F32, name="third")
+        final = psum.tile([P, P], F32, name="final")
+        sums = [early[:, 0:P], early[:, P : 2 * P], third[:], final[:]]
+
+        gather_and_turn(BLOCKS, v_grouped[0][:])
+        g_codes = pools.tile([P, E], U32, name="g_codes", tag="window%d" % BLOCKS, align_bytes=ALIGN)
+        g_scales = keep.tile([P, E], U8, name="g_scales", align_bytes=ALIGN)
+        gate_sums = psum.tile([P, E], F32, name="gate_sums")
+        multiply(gate_sums[:], g_grouped[:], g_codes[:], g_scales[:])
+        gate = keep.tile([P, E], F32, name="gate")
+        nc.scalar.activation(gate[:], gate_sums[:], ACT.Sigmoid)
+
+        for b in range(1, BLOCKS):
+            gather_and_turn(BLOCKS + b, v_grouped[b][:])
+            if b == BLOCKS - 1:
+                codes = last.tile([P, P], U32, name="codes_third", offset=0, align_bytes=ALIGN)
+            else:
+                codes = pools.tile([P, P], U32, name="v_codes%d" % b, tag="window%d" % (BLOCKS + b), align_bytes=ALIGN)
+            multiply(sums[b - 1], v_grouped[b - 1][:], codes[:], v_scales[b - 1][:])
+
+        result = last.tile([P, 3 * P], F32, name="result", offset=1024, align_bytes=ALIGN)
+        nc.vector.tensor_tensor(result[:, 0 : 2 * P], early[:], gate[:, 0 : 2 * P], ALU.mult)
+        nc.vector.tensor_tensor(result[:, 2 * P : 3 * P], third[:], gate[:, 2 * P : 3 * P], ALU.mult)
+        nc.sync.dma_start(out[:, 0 : 3 * P], result[:])
+
+        codes_final = keep.tile([P, P], U32, name="codes_final", align_bytes=ALIGN)
+        multiply(sums[3], v_grouped[3][:], codes_final[:], v_scales[3][:])
+        result_final = keep.tile([P, P], F32, name="result_final")
+        nc.vector.tensor_tensor(result_final[:], final[:], gate[:, 3 * P : 4 * P], ALU.mult)
+        nc.sync.dma_start(out[:, 3 * P : 4 * P], result_final[:])

@@ -18,51 +18,57 @@ ALU = mybir.AluOpType
 
 P = 128
 PACK = 4
-BLOCKS = E // P
 ALIGN = 64
+HALF = 16
+MX_BLOCKS = I // 32
 
 
 def tile_attend_gatedvalues_kernel(tc, query, keys_words, keys_scales, size, vals, gval, offs, out):
     nc = tc.nc
     with ExitStack() as ctx:
         keep = ctx.enter_context(tc.tile_pool(name="keep", bufs=1))
-        pools = ctx.enter_context(tc.tile_pool(name="pools", bufs=1))
         last = ctx.enter_context(tc.tile_pool(name="last", bufs=1))
         ring = ctx.enter_context(tc.tile_pool(name="ring", bufs=2))
         psum = ctx.enter_context(tc.psum_pool(name="psum", bufs=1))
         turn = ctx.enter_context(tc.psum_pool(name="turn", bufs=2))
 
-        offsets = keep.tile([P, I // 16], U16, name="offsets")
-        nc.sync.dma_start(offsets[:], offs)
-
-        key_pool = keep.tile([P, T], U32, name="key_pool")
-        nc.sync.dma_start(key_pool[:].bitcast(I32), keys_words.rearrange("z p n t -> p (z n t)").bitcast(I32))
         q_raw = keep.tile([P, PACK, Q], F32, name="q_raw")
         nc.sync.dma_start(q_raw[:], query.rearrange("(p j) q -> p j q", j=PACK))
+        offsets = keep.tile([P, I // 16], U16, name="offsets")
+        nc.sync.dma_start(offsets[:], offs)
+        key_pool = keep.tile([P, T], U32, name="key_pool")
+        nc.sync.dma_start(key_pool[:].bitcast(I32), keys_words.rearrange("z p n t -> p (z n t)").bitcast(I32))
 
         size_col = keep.tile([P, PACK], F32, name="size_col")
         nc.scalar.dma_start(size_col[:], size.rearrange("o (p t) -> p (o t)", t=PACK))
         scale_pool = keep.tile([P, T], U8, name="scale_pool")
         nc.vector.memset(scale_pool[:].bitcast(I32), 0)
         for quad in range(4):
-            nc.scalar.dma_start(
+            nc.sync.dma_start(
                 scale_pool[32 * quad : 32 * quad + 4, :].bitcast(I32),
                 keys_scales[0, 4 * quad : 4 * quad + 4, :].bitcast(I32),
             )
 
-        windows = []
-        for n in range(2 * BLOCKS):
-            source = gval if n < BLOCKS else vals
-            rows = source[(n % BLOCKS) * P : (n % BLOCKS + 1) * P, :]
-            if n == 2 * BLOCKS - 1:
-                window = last.tile([P, T], F32, name="window_last", offset=0, align_bytes=ALIGN)
-            else:
-                window = pools.tile([P, T], F32, name="window%d" % n, tag="window%d" % n, align_bytes=ALIGN)
-            nc.sync.dma_start(window[:], rows)
-            windows.append(window)
+        def load_pair(source, first, name):
+            pair = keep.tile([P, 2, T], F32, name=name)
+            nc.sync.dma_start(pair[:], source[first * P : (first + 2) * P, :].rearrange("(j p) t -> p j t", p=P))
+            return [pair[:, 0, :], pair[:, 1, :]]
+
+        gate_windows = load_pair(gval, 0, "gval_low") + load_pair(gval, 2, "gval_high")
+        value_windows = load_pair(vals, 0, "vals_low")
+        vals_third = keep.tile([P, T], F32, name="vals_third", tag="third", align_bytes=ALIGN)
+        nc.sync.dma_start(vals_third[:], vals[2 * P : 3 * P, :])
+        vals_last = last.tile([P, T], F32, name="vals_last", offset=0, align_bytes=ALIGN)
+        nc.sync.dma_start(vals_last[:], vals[3 * P : 4 * P, :])
 
         ident = keep.tile([P, P], F32, name="ident")
         make_identity(nc, ident[:])
+
+        size_rows = psum.tile([P, PACK, P], F32, name="size_rows")
+        for t in range(PACK):
+            nc.tensor.transpose(size_rows[:, t, :], size_col[:, t : t + 1].to_broadcast([P, P]), ident[:])
+        size_dealt = keep.tile([P, 2, MX_BLOCKS, 4, PACK], F32, name="size_dealt")
+        nc.scalar.copy(size_dealt[:], size_rows[:].rearrange("q t (b u n) -> q u b n t", u=2, n=4))
 
         q_grouped = keep.tile([P, Q, PACK], BF16, name="q_grouped", align_bytes=ALIGN)
         nc.vector.tensor_copy(q_grouped[:], q_raw[:].rearrange("p j q -> p q j"))
@@ -75,37 +81,38 @@ def tile_attend_gatedvalues_kernel(tc, query, keys_words, keys_scales, size, val
         k_scales = keep.tile([P, I], U8, name="k_scales", align_bytes=ALIGN)
         nc.vector.tensor_copy(k_scales[:], scale_pool[:].indirect(offsets[:]))
 
-        scores = psum.tile([P, I], F32, name="scores", tag="soft")
+        def turn_slots(dealt, grouped):
+            words = dealt.bitcast(F32)
+            turned = turn.tile([P, 2, P], F32, name="turned")
+            for u in range(2):
+                nc.tensor.transpose(turned[:, u, :], words[:, u * P : (u + 1) * P], ident[:])
+            nc.scalar.copy(grouped.bitcast(F32).rearrange("s (e u) -> s e u", u=2), turned[:].rearrange("s u e -> s e u"))
+
+        scores = psum.tile([P, I], F32, name="scores")
         nc.tensor.matmul_mx(scores[:], q_codes[:].bitcast(FP8X4), q_scales[:], k_codes[:].bitcast(FP8X4), k_scales[:],
                             start=True, stop=True)
         neg_max = keep.tile([P, 1], F32, name="neg_max")
         nc.vector.tensor_reduce(neg_max[:], scores[:], mybir.AxisListType.X, ALU.max, negate=True)
-        expo = keep.tile([P, PACK, P], F32, name="expo")
+        expo = keep.tile([P, I], F32, name="expo")
         row_sum = keep.tile([P, 1], F32, name="row_sum")
-        nc.scalar.activation(expo[:], scores[:].rearrange("q (s t) -> q t s", t=PACK), ACT.Exp, bias=neg_max[:],
+        nc.scalar.activation(expo[:].rearrange("q (u b x) -> q u b x", u=2, x=HALF),
+                             scores[:].rearrange("q (b u x) -> q u b x", u=2, x=HALF), ACT.Exp, bias=neg_max[:],
                              accum_out=row_sum[:])
         inv_sum = keep.tile([P, 1], F32, name="inv_sum")
         nc.vector.reciprocal(inv_sum[:], row_sum[:])
-        prob = keep.tile([P, PACK, P], F32, name="prob")
-        nc.scalar.activation(prob[:], expo[:], ACT.Copy, scale=inv_sum[:])
-        prob_t = psum.tile([P, PACK, Q], F32, name="prob_t", tag="soft")
-        for t in range(PACK):
-            nc.tensor.transpose(prob_t[:, t, :], prob[:, t, :], ident[:])
-        w_grouped = keep.tile([P, Q, PACK], BF16, name="w_grouped", align_bytes=ALIGN)
-        nc.vector.tensor_tensor(w_grouped[:], prob_t[:].rearrange("s t q -> s q t"),
-                                size_col[:].unsqueeze(1).to_broadcast([P, Q, PACK]), ALU.mult)
+        w_dealt = keep.tile([P, I], BF16, name="w_dealt")
+        nc.vector.scalar_tensor_tensor(w_dealt[:], expo[:], inv_sum[:],
+                                       size_dealt[:].rearrange("q u b n t -> q (u b n t)"), ALU.mult, ALU.mult)
+        w_grouped = keep.tile([P, Q * PACK], BF16, name="w_grouped", align_bytes=ALIGN)
+        turn_slots(w_dealt[:], w_grouped[:])
         w_codes = keep.tile([P, Q], U32, name="w_codes", align_bytes=ALIGN)
         w_scales = keep.tile([P, Q], U8, name="w_scales", align_bytes=ALIGN)
-        nc.vector.quantize_mx(w_codes[:].bitcast(FP8X4), w_scales[:], w_grouped[:].rearrange("p q j -> p (q j)"))
+        nc.vector.quantize_mx(w_codes[:].bitcast(FP8X4), w_scales[:], w_grouped[:])
 
-        def gather_and_turn(n, grouped):
+        def gather_and_turn(window, grouped):
             picked = ring.tile([P, I], BF16, name="picked")
-            nc.vector.tensor_copy(picked[:], windows[n][:].indirect(offsets[:]))
-            words = picked[:].bitcast(F32)
-            turned = turn.tile([P, 2, P], F32, name="turned")
-            for u in range(2):
-                nc.tensor.transpose(turned[:, u, :], words[:, u : I // 2 : 2], ident[:])
-            nc.scalar.copy(grouped.bitcast(F32).rearrange("s (e u) -> s e u", u=2), turned[:].rearrange("s u e -> s e u"))
+            nc.vector.tensor_copy(picked[:].rearrange("e (u b x) -> e b u x", u=2, x=HALF), window.indirect(offsets[:]))
+            turn_slots(picked[:], grouped)
 
         def multiply(sums, grouped, codes, scales):
             nc.vector.quantize_mx(codes.bitcast(FP8X4), scales, grouped)
@@ -113,39 +120,43 @@ def tile_attend_gatedvalues_kernel(tc, query, keys_words, keys_scales, size, val
                                 start=True, stop=True)
 
         g_grouped = keep.tile([P, E * PACK], BF16, name="g_grouped", align_bytes=ALIGN)
-        for n in range(BLOCKS):
-            gather_and_turn(n, g_grouped[:, n * P * PACK : (n + 1) * P * PACK])
-
-        v_grouped = [keep.tile([P, P * PACK], BF16, name="v_grouped%d" % b, align_bytes=ALIGN) for b in range(BLOCKS)]
-        v_scales = [keep.tile([P, P], U8, name="v_scales%d" % b, align_bytes=ALIGN) for b in range(BLOCKS)]
-        early = psum.tile([P, 2 * P], F32, name="early")
-        third = psum.tile([P, P], F32, name="third")
-        final = psum.tile([P, P], F32, name="final")
-        sums = [early[:, 0:P], early[:, P : 2 * P], third[:], final[:]]
-
-        gather_and_turn(BLOCKS, v_grouped[0][:])
-        g_codes = pools.tile([P, E], U32, name="g_codes", tag="window%d" % BLOCKS, align_bytes=ALIGN)
+        for n in range(4):
+            gather_and_turn(gate_windows[n], g_grouped[:, n * P * PACK : (n + 1) * P * PACK])
+        g_codes = keep.tile([P, E], U32, name="g_codes", align_bytes=ALIGN)
         g_scales = keep.tile([P, E], U8, name="g_scales", align_bytes=ALIGN)
         gate_sums = psum.tile([P, E], F32, name="gate_sums")
         multiply(gate_sums[:], g_grouped[:], g_codes[:], g_scales[:])
         gate = keep.tile([P, E], F32, name="gate")
         nc.scalar.activation(gate[:], gate_sums[:], ACT.Sigmoid)
 
-        for b in range(1, BLOCKS):
-            gather_and_turn(BLOCKS + b, v_grouped[b][:])
-            if b == BLOCKS - 1:
-                codes = last.tile([P, P], U32, name="codes_third", offset=0, align_bytes=ALIGN)
-            else:
-                codes = pools.tile([P, P], U32, name="v_codes%d" % b, tag="window%d" % (BLOCKS + b), align_bytes=ALIGN)
-            multiply(sums[b - 1], v_grouped[b - 1][:], codes[:], v_scales[b - 1][:])
+        low_grouped = keep.tile([P, 2 * P * PACK], BF16, name="low_grouped", align_bytes=ALIGN)
+        for n in range(2):
+            gather_and_turn(value_windows[n], low_grouped[:, n * P * PACK : (n + 1) * P * PACK])
+        third_grouped = keep.tile([P, P * PACK], BF16, name="third_grouped", align_bytes=ALIGN)
+        gather_and_turn(vals_third[:], third_grouped[:])
+
+        low_codes = keep.tile([P, 2 * P], U32, name="low_codes", tag="third", align_bytes=ALIGN)
+        low_scales = keep.tile([P, 2 * P], U8, name="low_scales", align_bytes=ALIGN)
+        low_sums = psum.tile([P, 2 * P], F32, name="low_sums")
+        multiply(low_sums[:], low_grouped[:], low_codes[:], low_scales[:])
+
+        last_grouped = keep.tile([P, P * PACK], BF16, name="last_grouped", align_bytes=ALIGN)
+        gather_and_turn(vals_last[:], last_grouped[:])
+
+        third_codes = last.tile([P, P], U32, name="third_codes", offset=0, align_bytes=ALIGN)
+        third_scales = keep.tile([P, P], U8, name="third_scales", align_bytes=ALIGN)
+        third_sums = psum.tile([P, P], F32, name="third_sums")
+        multiply(third_sums[:], third_grouped[:], third_codes[:], third_scales[:])
 
         result = last.tile([P, 3 * P], F32, name="result", offset=1024, align_bytes=ALIGN)
-        nc.vector.tensor_tensor(result[:, 0 : 2 * P], early[:], gate[:, 0 : 2 * P], ALU.mult)
-        nc.vector.tensor_tensor(result[:, 2 * P : 3 * P], third[:], gate[:, 2 * P : 3 * P], ALU.mult)
+        nc.vector.tensor_tensor(result[:, 0 : 2 * P], low_sums[:], gate[:, 0 : 2 * P], ALU.mult)
+        nc.vector.tensor_tensor(result[:, 2 * P : 3 * P], third_sums[:], gate[:, 2 * P : 3 * P], ALU.mult)
         nc.sync.dma_start(out[:, 0 : 3 * P], result[:])
 
-        codes_final = keep.tile([P, P], U32, name="codes_final", align_bytes=ALIGN)
-        multiply(sums[3], v_grouped[3][:], codes_final[:], v_scales[3][:])
-        result_final = keep.tile([P, P], F32, name="result_final")
-        nc.vector.tensor_tensor(result_final[:], final[:], gate[:, 3 * P : 4 * P], ALU.mult)
-        nc.sync.dma_start(out[:, 3 * P : 4 * P], result_final[:])
+        last_codes = keep.tile([P, P], U32, name="last_codes", align_bytes=ALIGN)
+        last_scales = keep.tile([P, P], U8, name="last_scales", align_bytes=ALIGN)
+        last_sums = psum.tile([P, P], F32, name="last_sums")
+        multiply(last_sums[:], last_grouped[:], last_codes[:], last_scales[:])
+        result_last = keep.tile([P, P], F32, name="result_last")
+        nc.vector.tensor_tensor(result_last[:], last_sums[:], gate[:, 3 * P : 4 * P], ALU.mult)
+        nc.sync.dma_start(out[:, 3 * P : 4 * P], result_last[:])

@@ -28,19 +28,19 @@ def tile_attend_gatedvalues_kernel(tc, query, keys_words, keys_scales, size, val
     with ExitStack() as ctx:
         keep = ctx.enter_context(tc.tile_pool(name="keep", bufs=1))
         last = ctx.enter_context(tc.tile_pool(name="last", bufs=1))
-        ring = ctx.enter_context(tc.tile_pool(name="ring", bufs=2))
+        ring = ctx.enter_context(tc.tile_pool(name="ring", bufs=3))
         psum = ctx.enter_context(tc.psum_pool(name="psum", bufs=1))
         turn = ctx.enter_context(tc.psum_pool(name="turn", bufs=2))
 
-        q_raw = keep.tile([P, PACK, Q], F32, name="q_raw")
-        nc.sync.dma_start(q_raw[:], query.rearrange("(p j) q -> p j q", j=PACK))
         offsets = keep.tile([P, I // 16], U16, name="offsets")
         nc.sync.dma_start(offsets[:], offs)
-        key_pool = keep.tile([P, T], U32, name="key_pool")
-        nc.sync.dma_start(key_pool[:].bitcast(I32), keys_words.rearrange("z p n t -> p (z n t)").bitcast(I32))
-
         size_col = keep.tile([P, PACK], F32, name="size_col")
         nc.scalar.dma_start(size_col[:], size.rearrange("o (p t) -> p (o t)", t=PACK))
+        key_pool = keep.tile([P, T], U32, name="key_pool")
+        nc.sync.dma_start(key_pool[:].bitcast(I32), keys_words.rearrange("z p n t -> p (z n t)").bitcast(I32))
+        q_raw = keep.tile([P, PACK, Q], F32, name="q_raw")
+        nc.sync.dma_start(q_raw[:], query.rearrange("(p j) q -> p j q", j=PACK))
+
         scale_pool = keep.tile([P, T], U8, name="scale_pool")
         nc.vector.memset(scale_pool[:].bitcast(I32), 0)
         for quad in range(4):
@@ -50,12 +50,16 @@ def tile_attend_gatedvalues_kernel(tc, query, keys_words, keys_scales, size, val
             )
 
         def load_pair(source, first, name):
-            pair = keep.tile([P, 2, T], F32, name=name)
+            pair = keep.tile([P, 2, T], F32, name=name, tag=name, align_bytes=ALIGN)
             nc.sync.dma_start(pair[:], source[first * P : (first + 2) * P, :].rearrange("(j p) t -> p j t", p=P))
             return [pair[:, 0, :], pair[:, 1, :]]
 
         gate_windows = load_pair(gval, 0, "gval_low") + load_pair(gval, 2, "gval_high")
-        value_windows = load_pair(vals, 0, "vals_low")
+        value_windows = []
+        for n in range(2):
+            window = keep.tile([P, T], F32, name="vals%d" % n, tag="vals%d" % n, align_bytes=ALIGN)
+            nc.sync.dma_start(window[:], vals[n * P : (n + 1) * P, :])
+            value_windows.append(window[:])
         vals_third = keep.tile([P, T], F32, name="vals_third", tag="third", align_bytes=ALIGN)
         nc.sync.dma_start(vals_third[:], vals[2 * P : 3 * P, :])
         vals_last = last.tile([P, T], F32, name="vals_last", offset=0, align_bytes=ALIGN)
@@ -71,7 +75,7 @@ def tile_attend_gatedvalues_kernel(tc, query, keys_words, keys_scales, size, val
         nc.scalar.copy(size_dealt[:], size_rows[:].rearrange("q t (b u n) -> q u b n t", u=2, n=4))
 
         q_grouped = keep.tile([P, Q, PACK], BF16, name="q_grouped", align_bytes=ALIGN)
-        nc.vector.tensor_copy(q_grouped[:], q_raw[:].rearrange("p j q -> p q j"))
+        nc.scalar.copy(q_grouped[:], q_raw[:].rearrange("p j q -> p q j"))
         q_codes = keep.tile([P, Q], U32, name="q_codes", align_bytes=ALIGN)
         q_scales = keep.tile([P, Q], U8, name="q_scales", align_bytes=ALIGN)
         nc.vector.quantize_mx(q_codes[:].bitcast(FP8X4), q_scales[:], q_grouped[:].rearrange("p q j -> p (q j)"))
@@ -105,10 +109,6 @@ def tile_attend_gatedvalues_kernel(tc, query, keys_words, keys_scales, size, val
                                        size_dealt[:].rearrange("q u b n t -> q (u b n t)"), ALU.mult, ALU.mult)
         w_grouped = keep.tile([P, Q * PACK], BF16, name="w_grouped", align_bytes=ALIGN)
         turn_slots(w_dealt[:], w_grouped[:])
-        w_codes = keep.tile([P, Q], U32, name="w_codes", align_bytes=ALIGN)
-        w_scales = keep.tile([P, Q], U8, name="w_scales", align_bytes=ALIGN)
-        nc.vector.quantize_mx(w_codes[:].bitcast(FP8X4), w_scales[:], w_grouped[:])
-
         def gather_and_turn(window, grouped):
             picked = ring.tile([P, I], BF16, name="picked")
             nc.vector.tensor_copy(picked[:].rearrange("e (u b x) -> e b u x", u=2, x=HALF), window.indirect(offsets[:]))
@@ -120,18 +120,25 @@ def tile_attend_gatedvalues_kernel(tc, query, keys_words, keys_scales, size, val
                                 start=True, stop=True)
 
         g_grouped = keep.tile([P, E * PACK], BF16, name="g_grouped", align_bytes=ALIGN)
-        for n in range(4):
+        for n in range(2):
             gather_and_turn(gate_windows[n], g_grouped[:, n * P * PACK : (n + 1) * P * PACK])
-        g_codes = keep.tile([P, E], U32, name="g_codes", align_bytes=ALIGN)
+        w_codes = keep.tile([P, Q], U32, name="w_codes", tag="gval_low", align_bytes=ALIGN)
+        w_scales = keep.tile([P, Q], U8, name="w_scales", align_bytes=ALIGN)
+        nc.vector.quantize_mx(w_codes[:].bitcast(FP8X4), w_scales[:], w_grouped[:])
+        for n in range(2, 4):
+            gather_and_turn(gate_windows[n], g_grouped[:, n * P * PACK : (n + 1) * P * PACK])
+        low_grouped = keep.tile([P, 2 * P * PACK], BF16, name="low_grouped", align_bytes=ALIGN)
+        gather_and_turn(value_windows[0], low_grouped[:, 0 : P * PACK])
+        g_codes = keep.tile([P, E], U32, name="g_codes", tag="vals0", align_bytes=ALIGN)
         g_scales = keep.tile([P, E], U8, name="g_scales", align_bytes=ALIGN)
         gate_sums = psum.tile([P, E], F32, name="gate_sums")
         multiply(gate_sums[:], g_grouped[:], g_codes[:], g_scales[:])
+        gate_tanh = keep.tile([P, E], F32, name="gate_tanh")
+        nc.scalar.activation(gate_tanh[:], gate_sums[:], ACT.Tanh, scale=0.5)
         gate = keep.tile([P, E], F32, name="gate")
-        nc.scalar.activation(gate[:], gate_sums[:], ACT.Sigmoid)
+        nc.scalar.activation(gate[:], gate_tanh[:], ACT.Copy, scale=0.5, bias=0.5)
 
-        low_grouped = keep.tile([P, 2 * P * PACK], BF16, name="low_grouped", align_bytes=ALIGN)
-        for n in range(2):
-            gather_and_turn(value_windows[n], low_grouped[:, n * P * PACK : (n + 1) * P * PACK])
+        gather_and_turn(value_windows[1], low_grouped[:, P * PACK : 2 * P * PACK])
         third_grouped = keep.tile([P, P * PACK], BF16, name="third_grouped", align_bytes=ALIGN)
         gather_and_turn(vals_third[:], third_grouped[:])
 

@@ -32,22 +32,19 @@ def tile_attend_gatedvalues_kernel(tc, query, keys_words, keys_scales, size, val
         psum = ctx.enter_context(tc.psum_pool(name="psum", bufs=1))
         turn = ctx.enter_context(tc.psum_pool(name="turn", bufs=2))
 
+        q_raw = keep.tile([P, PACK, Q], F32, name="q_raw")
+        nc.sync.dma_start(q_raw[:], query.rearrange("(p j) q -> p j q", j=PACK))
         offsets = keep.tile([P, I // 16], U16, name="offsets")
         nc.sync.dma_start(offsets[:], offs)
         size_col = keep.tile([P, PACK], F32, name="size_col")
-        nc.scalar.dma_start(size_col[:], size.rearrange("o (p t) -> p (o t)", t=PACK))
+        nc.sync.dma_start(size_col[:], size.rearrange("o (p t) -> p (o t)", t=PACK))
         key_pool = keep.tile([P, T], U32, name="key_pool")
         nc.sync.dma_start(key_pool[:].bitcast(I32), keys_words.rearrange("z p n t -> p (z n t)").bitcast(I32))
-        q_raw = keep.tile([P, PACK, Q], F32, name="q_raw")
-        nc.sync.dma_start(q_raw[:], query.rearrange("(p j) q -> p j q", j=PACK))
 
         scale_pool = keep.tile([P, T], U8, name="scale_pool")
         nc.vector.memset(scale_pool[:].bitcast(I32), 0)
-        for quad in range(4):
-            nc.sync.dma_start(
-                scale_pool[32 * quad : 32 * quad + 4, :].bitcast(I32),
-                keys_scales[0, 4 * quad : 4 * quad + 4, :].bitcast(I32),
-            )
+        for r in range(4):
+            nc.sync.dma_start(scale_pool[r:P:32, :].bitcast(I32), keys_scales[0, r:16:4, :].bitcast(I32))
 
         def load_pair(source, first, name):
             pair = keep.tile([P, 2, T], F32, name=name, tag=name, align_bytes=ALIGN)

from contextlib import ExitStack

import concourse.mybir as mybir
from concourse.masks import make_identity

D, T, I, Q, E = 512, 2048, 512, 128, 512
FLOPS = 2 * Q * I * (D + 2 * E)

F32 = mybir.dt.float32
BF16 = mybir.dt.bfloat16
I32 = mybir.dt.int32
U32 = mybir.dt.uint32
U16 = mybir.dt.uint16
U8 = mybir.dt.uint8
FP8X4 = mybir.dt.float8_e4m3fn_x4
ACT = mybir.ActivationFunctionType
ALU = mybir.AluOpType

P = 128
PACK = 4
ALIGN = 64
HALF = 16
MX_BLOCKS = I // 32


def tile_attend_gatedvalues_kernel(tc, query, keys_words, keys_scales, size, vals, gval, offs, out):
    nc = tc.nc
    with ExitStack() as ctx:
        keep = ctx.enter_context(tc.tile_pool(name="keep", bufs=1))
        last = ctx.enter_context(tc.tile_pool(name="last", bufs=1))
        ring = ctx.enter_context(tc.tile_pool(name="ring", bufs=3))
        psum = ctx.enter_context(tc.psum_pool(name="psum", bufs=1))
        turn = ctx.enter_context(tc.psum_pool(name="turn", bufs=2))

        q_raw = keep.tile([P, PACK, Q], F32, name="q_raw")
        nc.sync.dma_start(q_raw[:], query.rearrange("(p j) q -> p j q", j=PACK))
        offsets = keep.tile([P, I // 16], U16, name="offsets")
        nc.sync.dma_start(offsets[:], offs)
        size_col = keep.tile([P, PACK], F32, name="size_col")
        nc.sync.dma_start(size_col[:], size.rearrange("o (p t) -> p (o t)", t=PACK))
        key_pool = keep.tile([P, T], U32, name="key_pool")
        nc.sync.dma_start(key_pool[:].bitcast(I32), keys_words.rearrange("z p n t -> p (z n t)").bitcast(I32))

        scale_pool = keep.tile([P, T], U8, name="scale_pool")
        nc.vector.memset(scale_pool[:].bitcast(I32), 0)
        for r in range(4):
            nc.sync.dma_start(scale_pool[r:P:32, :].bitcast(I32), keys_scales[0, r:16:4, :].bitcast(I32))

        def load_pair(source, first, name):
            pair = keep.tile([P, 2, T], F32, name=name, tag=name, align_bytes=ALIGN)
            nc.sync.dma_start(pair[:], source[first * P : (first + 2) * P, :].rearrange("(j p) t -> p j t", p=P))
            return [pair[:, 0, :], pair[:, 1, :]]

        gate_windows = load_pair(gval, 0, "gval_low") + load_pair(gval, 2, "gval_high")
        value_windows = []
        for n in range(2):
            window = keep.tile([P, T], F32, name="vals%d" % n, tag="vals%d" % n, align_bytes=ALIGN)
            nc.sync.dma_start(window[:], vals[n * P : (n + 1) * P, :])
            value_windows.append(window[:])
        vals_third = keep.tile([P, T], F32, name="vals_third", tag="third", align_bytes=ALIGN)
        nc.sync.dma_start(vals_third[:], vals[2 * P : 3 * P, :])
        vals_last = last.tile([P, T], F32, name="vals_last", offset=0, align_bytes=ALIGN)
        nc.sync.dma_start(vals_last[:], vals[3 * P : 4 * P, :])

        ident = keep.tile([P, P], F32, name="ident")
        make_identity(nc, ident[:])

        size_rows = psum.tile([P, PACK, P], F32, name="size_rows")
        for t in range(PACK):
            nc.tensor.transpose(size_rows[:, t, :], size_col[:, t : t + 1].to_broadcast([P, P]), ident[:])
        size_dealt = keep.tile([P, 2, MX_BLOCKS, 4, PACK], F32, name="size_dealt")
        nc.scalar.copy(size_dealt[:], size_rows[:].rearrange("q t (b u n) -> q u b n t", u=2, n=4))

        q_grouped = keep.tile([P, Q, PACK], BF16, name="q_grouped", align_bytes=ALIGN)
        nc.scalar.copy(q_grouped[:], q_raw[:].rearrange("p j q -> p q j"))
        q_codes = keep.tile([P, Q], U32, name="q_codes", align_bytes=ALIGN)
        q_scales = keep.tile([P, Q], U8, name="q_scales", align_bytes=ALIGN)
        nc.vector.quantize_mx(q_codes[:].bitcast(FP8X4), q_scales[:], q_grouped[:].rearrange("p q j -> p (q j)"))

        k_codes = keep.tile([P, I], U32, name="k_codes", align_bytes=ALIGN)
        nc.vector.tensor_copy(k_codes[:], key_pool[:].indirect(offsets[:]))
        k_scales = keep.tile([P, I], U8, name="k_scales", align_bytes=ALIGN)
        nc.vector.tensor_copy(k_scales[:], scale_pool[:].indirect(offsets[:]))

        def turn_slots(dealt, grouped):
            words = dealt.bitcast(F32)
            turned = turn.tile([P, 2, P], F32, name="turned")
            for u in range(2):
                nc.tensor.transpose(turned[:, u, :], words[:, u * P : (u + 1) * P], ident[:])
            nc.scalar.copy(grouped.bitcast(F32).rearrange("s (e u) -> s e u", u=2), turned[:].rearrange("s u e -> s e u"))

        scores = psum.tile([P, I], F32, name="scores")
        nc.tensor.matmul_mx(scores[:], q_codes[:].bitcast(FP8X4), q_scales[:], k_codes[:].bitcast(FP8X4), k_scales[:],
                            start=True, stop=True)
        neg_max = keep.tile([P, 1], F32, name="neg_max")
        nc.vector.tensor_reduce(neg_max[:], scores[:], mybir.AxisListType.X, ALU.max, negate=True)
        expo = keep.tile([P, I], F32, name="expo")
        row_sum = keep.tile([P, 1], F32, name="row_sum")
        nc.scalar.activation(expo[:].rearrange("q (u b x) -> q u b x", u=2, x=HALF),
                             scores[:].rearrange("q (b u x) -> q u b x", u=2, x=HALF), ACT.Exp, bias=neg_max[:],
                             accum_out=row_sum[:])
        inv_sum = keep.tile([P, 1], F32, name="inv_sum")
        nc.vector.reciprocal(inv_sum[:], row_sum[:])
        w_dealt = keep.tile([P, I], BF16, name="w_dealt")
        nc.vector.scalar_tensor_tensor(w_dealt[:], expo[:], inv_sum[:],
                                       size_dealt[:].rearrange("q u b n t -> q (u b n t)"), ALU.mult, ALU.mult)
        w_grouped = keep.tile([P, Q * PACK], BF16, name="w_grouped", align_bytes=ALIGN)
        turn_slots(w_dealt[:], w_grouped[:])
        def gather_and_turn(window, grouped):
            picked = ring.tile([P, I], BF16, name="picked")
            nc.vector.tensor_copy(picked[:].rearrange("e (u b x) -> e b u x", u=2, x=HALF), window.indirect(offsets[:]))
            turn_slots(picked[:], grouped)

        def multiply(sums, grouped, codes, scales):
            nc.vector.quantize_mx(codes.bitcast(FP8X4), scales, grouped)
            nc.tensor.matmul_mx(sums, w_codes[:].bitcast(FP8X4), w_scales[:], codes.bitcast(FP8X4), scales,
                                start=True, stop=True)

        g_grouped = keep.tile([P, E * PACK], BF16, name="g_grouped", align_bytes=ALIGN)
        for n in range(2):
            gather_and_turn(gate_windows[n], g_grouped[:, n * P * PACK : (n + 1) * P * PACK])
        w_codes = keep.tile([P, Q], U32, name="w_codes", tag="gval_low", align_bytes=ALIGN)
        w_scales = keep.tile([P, Q], U8, name="w_scales", align_bytes=ALIGN)
        nc.vector.quantize_mx(w_codes[:].bitcast(FP8X4), w_scales[:], w_grouped[:])
        for n in range(2, 4):
            gather_and_turn(gate_windows[n], g_grouped[:, n * P * PACK : (n + 1) * P * PACK])
        low_grouped = keep.tile([P, 2 * P * PACK], BF16, name="low_grouped", align_bytes=ALIGN)
        gather_and_turn(value_windows[0], low_grouped[:, 0 : P * PACK])
        g_codes = keep.tile([P, E], U32, name="g_codes", tag="vals0", align_bytes=ALIGN)
        g_scales = keep.tile([P, E], U8, name="g_scales", align_bytes=ALIGN)
        gate_sums = psum.tile([P, E], F32, name="gate_sums")
        multiply(gate_sums[:], g_grouped[:], g_codes[:], g_scales[:])
        gate_tanh = keep.tile([P, E], F32, name="gate_tanh")
        nc.scalar.activation(gate_tanh[:], gate_sums[:], ACT.Tanh, scale=0.5)
        gate = keep.tile([P, E], F32, name="gate")
        nc.scalar.activation(gate[:], gate_tanh[:], ACT.Copy, scale=0.5, bias=0.5)

        gather_and_turn(value_windows[1], low_grouped[:, P * PACK : 2 * P * PACK])
        third_grouped = keep.tile([P, P * PACK], BF16, name="third_grouped", align_bytes=ALIGN)
        gather_and_turn(vals_third[:], third_grouped[:])

        low_codes = keep.tile([P, 2 * P], U32, name="low_codes", tag="third", align_bytes=ALIGN)
        low_scales = keep.tile([P, 2 * P], U8, name="low_scales", align_bytes=ALIGN)
        low_sums = psum.tile([P, 2 * P], F32, name="low_sums")
        multiply(low_sums[:], low_grouped[:], low_codes[:], low_scales[:])

        last_grouped = keep.tile([P, P * PACK], BF16, name="last_grouped", align_bytes=ALIGN)
        gather_and_turn(vals_last[:], last_grouped[:])

        third_codes = last.tile([P, P], U32, name="third_codes", offset=0, align_bytes=ALIGN)
        third_scales = keep.tile([P, P], U8, name="third_scales", align_bytes=ALIGN)
        third_sums = psum.tile([P, P], F32, name="third_sums")
        multiply(third_sums[:], third_grouped[:], third_codes[:], third_scales[:])

        result = last.tile([P, 3 * P], F32, name="result", offset=1024, align_bytes=ALIGN)
        nc.vector.tensor_tensor(result[:, 0 : 2 * P], low_sums[:], gate[:, 0 : 2 * P], ALU.mult)
        nc.vector.tensor_tensor(result[:, 2 * P : 3 * P], third_sums[:], gate[:, 2 * P : 3 * P], ALU.mult)
        nc.sync.dma_start(out[:, 0 : 3 * P], result[:])

        last_codes = keep.tile([P, P], U32, name="last_codes", align_bytes=ALIGN)
        last_scales = keep.tile([P, P], U8, name="last_scales", align_bytes=ALIGN)
        last_sums = psum.tile([P, P], F32, name="last_sums")
        multiply(last_sums[:], last_grouped[:], last_codes[:], last_scales[:])
        result_last = keep.tile([P, P], F32, name="result_last")
        nc.vector.tensor_tensor(result_last[:], last_sums[:], gate[:, 3 * P : 4 * P], ALU.mult)
        nc.sync.dma_start(out[:, 3 * P : 4 * P], result_last[:])
